import numpy as np
import ml_dtypes


def mxq(x, axis, fmt="e4m3"):
    dtype, down = {"e4m3": (ml_dtypes.float8_e4m3fn, 7), "e5m2": (ml_dtypes.float8_e5m2, 14)}[fmt]
    v = np.moveaxis(np.asarray(x, np.float32).astype(ml_dtypes.bfloat16).astype(np.float64), axis, -1)
    blocks = v.reshape(v.shape[:-1] + (-1, 32))
    amax = np.abs(blocks).max(-1, keepdims=True)
    byte = np.maximum(np.where(amax > 0, np.frexp(amax)[1] - 1 + 127, 0) - down, 1)
    scale = np.exp2(byte - 127.0)
    codes = (blocks / scale).astype(np.float32).astype(dtype).astype(np.float64)
    return np.moveaxis((codes * scale).reshape(v.shape), -1, axis)


WIDE = False


def mx_kscale(k):
    if not WIDE:
        return np.ones(k)
    levels = np.array([10, -10, 5, -5, 0])
    if k % 512:
        return np.exp2(np.random.permutation(np.resize(levels, k // 32))).repeat(32)
    a = np.empty((k // 512, 16))
    for p in range(k // 512):
        a[p, :8] = np.random.permutation(np.resize(levels, 8))
        for g in range(8):
            far = levels[np.abs(levels - a[p, g]) >= 10]
            a[p, g + 8] = far[np.random.randint(len(far))]
    return np.exp2(a.ravel()).repeat(32)


BF16 = ml_dtypes.bfloat16


def bf(x):
    return np.asarray(x, np.float32).astype(BF16)


def f64(x):
    return np.asarray(x).astype(np.float64)


B, L, R, D = 2, 1024, 2, 128


def time_gain(g, z):
    return g[None, :, None] * z


def time_mix(m, z):
    return mxq(m, 1, "e4m3") @ mxq(z, 1, "e4m3")


def draw0():
    s, u = mx_kscale(L), mx_kscale(L)
    root = np.sqrt(L)
    return {
        "x": bf(np.random.standard_normal((B, L, R, D))),
        "g1": bf((1.0 + 0.1 * np.random.standard_normal(L)) * s),
        "ma": bf(np.random.standard_normal((L, L)) / root / s[None, :]),
        "mc": bf(np.random.standard_normal((L, L)) / root / s[None, :]),
        "g2": bf((1.0 + 0.1 * np.random.standard_normal(L)) * u),
        "mu": bf(np.random.standard_normal((L, L)) / root / u[None, :]),
        "mv": bf(np.random.standard_normal((L, L)) / root / u[None, :]),
    }


def core(x, g1, ma, mc, g2, mu, mv):
    x = f64(x)
    g1, g2 = f64(g1), f64(g2)

    e = x[:, :, 0, :]
    o = x[:, :, 1, :]

    eg = time_gain(g1, e)
    og = time_gain(g1, o)

    pa = time_mix(f64(ma), og)
    pc = time_mix(f64(mc), eg)

    e1 = e * np.exp(np.tanh(pa))
    o1 = o * np.exp(np.tanh(pc))

    e1g = time_gain(g2, e1)
    o1g = time_gain(g2, o1)

    pu = time_mix(f64(mu), o1g)
    pv = time_mix(f64(mv), e1g)

    e2 = e1 + np.tanh(pu)
    o2 = o1 - np.tanh(pv)
    return e2, o2


def e4m3fn_bytes(y):
    return np.clip(np.asarray(y, np.float64), -448.0, 448.0).astype(np.float32).astype(ml_dtypes.float8_e4m3fn).view(np.uint8)


def e4m3fn_values(b):
    return np.asarray(b, np.uint8).view(ml_dtypes.float8_e4m3fn).astype(np.float64)


def setup_inputs():
    d = draw0()
    x0 = np.asarray(d['mv']).astype(np.float64)
    s = (np.max(np.abs(x0), axis=(0,), keepdims=True) / 448.0).astype(np.float32)
    out = {}
    for k, v in d.items():
        if k == 'mv':
            out['mv_bytes'] = e4m3fn_bytes(x0 / s.astype(np.float64))
            out['mv_scale'] = s
        else:
            out[k] = v
    return out


def reference(x, g1, ma, mc, g2, mu, mv_bytes, mv_scale):
    return core(x, g1, ma, mc, g2, mu, e4m3fn_values(mv_bytes) * mv_scale.astype(np.float64))

@@ -1,0 +1,274 @@
+from contextlib import ExitStack
+
+import concourse.mybir as mybir
+from concourse.masks import make_identity
+
+F32 = mybir.dt.float32
+BF16 = mybir.dt.bfloat16
+U32 = mybir.dt.uint32
+U8 = mybir.dt.uint8
+FP8 = mybir.dt.float8_e4m3fn
+FP8X4 = mybir.dt.float8_e4m3fn_x4
+ACT = mybir.ActivationFunctionType
+MULT = mybir.AluOpType.mult
+ADD = mybir.AluOpType.add
+SUB = mybir.AluOpType.subtract
+
+P = 128
+B, L, D = 2, 1024, 128
+G = 2
+J = 4
+C = B * D
+
+FLOPS = 4 * 2 * L * L * C
+
+
+def tile_scinetevenoddinteraction_kernel(tc, x, g1, ma, mc, g2, mu, mv_bytes, mv_scale, out_0, out_1):
+    nc = tc.nc
+    with ExitStack() as ctx:
+        keep = ctx.enter_context(tc.tile_pool(name="keep", bufs=1))
+        stage = ctx.enter_context(tc.tile_pool(name="stage", bufs=3))
+        tp_pool = ctx.enter_context(tc.psum_pool(name="tp", bufs=4))
+        acc_pool = ctx.enter_context(tc.psum_pool(name="acc", bufs=4))
+
+        def kept(name, shape, dtype):
+            return keep.tile(shape, dtype, name=name, align_bytes=64)
+
+        g1_t = kept("g1_t", [P, G, J], BF16)
+        g2_t = kept("g2_t", [P, G, J], BF16)
+        nc.scalar.dma_start(out=g1_t[:], in_=g1.rearrange("(g p j) -> p g j", p=P, j=J))
+        nc.scalar.dma_start(out=g2_t[:], in_=g2.rearrange("(g p j) -> p g j", p=P, j=J))
+        warm = kept("warm", [P, 1], F32)
+        nc.gpsimd.memset(warm[:], 0.0)
+        nc.scalar.activation(out=warm[:], in_=warm[:], func=ACT.Tanh)
+        ident = kept("ident", [P, P], F32)
+        make_identity(nc, ident[:])
+        ident_bf = kept("ident_bf", [P, P], BF16)
+        make_identity(nc, ident_bf[:])
+        diag = kept("diag", [P, G, J, P], BF16)
+        nc.vector.tensor_tensor(
+            out=diag[:].rearrange("p g j i -> p (g j) i"),
+            in0=ident_bf[:].unsqueeze(1).to_broadcast([P, G * J, P]),
+            in1=g1_t[:].rearrange("p g j -> p (g j)").unsqueeze(2).to_broadcast([P, G * J, P]),
+            op=MULT,
+        )
+
+        x_t = kept("x_t", [P, G, B, J, 2, D], BF16)
+        x_v = x.rearrange("b (g p j) h d -> g b p (j h d)", p=P, j=J)
+        raw = {}
+        pairs = [(m, g, q) for m in ("mc", "ma", "mu", "mv") for g in range(G) for q in range(2)]
+        for key in pairs:
+            raw[key] = kept("raw_%s_%d_%d" % key, [P, 2, L], BF16)
+        views = {n: a.rearrange("(g p j) k -> g p j k", p=P, j=J) for n, a in (("mc", mc), ("ma", ma), ("mu", mu))}
+
+        def load_pair(key):
+            m, g, q = key
+            nc.sync.dma_start(out=raw[key][:], in_=views[m][g, :, 2 * q : 2 * q + 2, :])
+
+        def load_x(g, b):
+            nc.sync.dma_start(out=x_t[:, g, b].rearrange("p j h d -> p (j h d)"), in_=x_v[g, b])
+
+        mvb = kept("mvb", [P, G, J, L], U8)
+        mvs = kept("mvs", [P, L], F32)
+        key = pairs[0]
+        for g in range(G):
+            for b in range(B):
+                load_x(g, b)
+            nc.sync.dma_start(out=raw[key][:, g, :], in_=views["mc"][0, :, g, :])
+        for key in pairs[1:6]:
+            load_pair(key)
+        nc.sync.dma_start(out=mvs[:], in_=mv_scale.rearrange("o k -> (o k)").partition_broadcast(P))
+        for g in range(G):
+            nc.sync.dma_start(out=mvb[:, g].rearrange("p j k -> p (j k)"), in_=mv_bytes.rearrange("(g p j) k -> g p (j k)", p=P, j=J)[g])
+        for key in pairs[6:12]:
+            load_pair(key)
+
+        def operand(name):
+            return (
+                kept(name + "_i", [P, G, C, J], BF16),
+                kept(name + "_c", [P, G, C], U32),
+                kept(name + "_s", [P, G, C], U8),
+            )
+
+        eg, og, e1g, o1g = operand("eg"), operand("og"), operand("e1g"), operand("o1g")
+
+        def quantize_operand(op, g):
+            inter, codes, scales = op
+            nc.vector.quantize_mx(
+                out=codes[:, g, :].bitcast(FP8X4), scales=scales[:, g, :], in_=inter[:, g].rearrange("p c j -> p (c j)")
+            )
+
+        def gain1_tensor(op, half, g):
+            bank = acc_pool.tile([P, J, C], BF16, name="gain_bank", tag="acc")
+            for j in range(J):
+                nc.tensor.matmul(
+                    out=bank[:, j, :].rearrange("p (b d) -> p b d", b=B),
+                    lhsT=diag[:, g, j, :],
+                    rhs=x_t[:, g, :, j, half, :],
+                    start=True,
+                    stop=True,
+                )
+            nc.scalar.copy(out=op[0][:, g], in_=bank[:].rearrange("p j c -> p c j"))
+
+        w_t, w_c, w_s, tp, acc = {}, {}, {}, {}, {}
+
+        def widen(key, r):
+            m, g, q = key
+            nc.vector.tensor_tensor(
+                out=raw[key][:, r, :], in0=mvb[:, g, 2 * q + r, :].bitcast(FP8), in1=mvs[:], op=MULT
+            )
+
+        def transpose(key):
+            words = raw[key][:].rearrange("p r k -> p (r k)").bitcast(F32)
+            for r in range(2):
+                bank = tp_pool.tile([P, G, 2, P], F32, name="tp_bank")
+                tp[key, r] = bank
+                for g in range(G):
+                    for u in range(2):
+                        k0 = 512 * r + 256 * g
+                        nc.tensor.transpose(bank[:, g, u, :], words[:, k0 + u : k0 + 256 : 2], ident[:])
+
+        def copy_out(key, engines):
+            w_t[key] = stage.tile([P, 2, G, P, J], BF16, name="w_t", align_bytes=64)
+            words = w_t[key][:].rearrange("p r g c j -> p (r g c j)").bitcast(F32)
+            for r in range(2):
+                o = words[:, 512 * r : 512 * (r + 1)].rearrange("p (g c u) -> p g c u", g=G, u=2)
+                i = tp[key, r][:].rearrange("p g u c -> p g c u")
+                if engines[r] == "S":
+                    nc.scalar.copy(out=o, in_=i)
+                else:
+                    nc.vector.tensor_copy(out=o, in_=i)
+
+        def quantize_rows(key, r):
+            if r == 0:
+                w_c[key] = stage.tile([P, 2 * G * P], U32, name="w_c", align_bytes=64, bufs=5)
+                w_s[key] = stage.tile([P, 2 * G * P], U8, name="w_s", align_bytes=64, bufs=5)
+            c0 = r * G * P
+            nc.vector.quantize_mx(
+                out=w_c[key][:, c0 : c0 + G * P].bitcast(FP8X4),
+                scales=w_s[key][:, c0 : c0 + G * P],
+                in_=w_t[key][:, r].rearrange("p g c j -> p (g c j)"),
+            )
+
+        def quantize_pair(key):
+            w_c[key] = stage.tile([P, 2 * G * P], U32, name="w_c", align_bytes=64, bufs=5)
+            w_s[key] = stage.tile([P, 2 * G * P], U8, name="w_s", align_bytes=64, bufs=5)
+            nc.vector.quantize_mx(
+                out=w_c[key][:].bitcast(FP8X4), scales=w_s[key][:], in_=w_t[key][:].rearrange("p r g c j -> p (r g c j)")
+            )
+
+        rhs_of = {"mc": eg, "ma": og, "mu": o1g, "mv": e1g}
+
+        def multiply(key, rows=(0, 1)):
+            codes, scales = rhs_of[key[0]][1:]
+            acc[key] = acc_pool.tile([P, 2, C], F32, name="acc_bank", tag="acc")
+            for r in rows:
+                for g in range(G):
+                    c0 = (r * G + g) * P
+                    nc.tensor.matmul_mx(
+                        out=acc[key][:, r, :],
+                        lhsT=w_c[key][:, c0 : c0 + P].bitcast(FP8X4),
+                        lhsT_scale=w_s[key][:, c0 : c0 + P],
+                        rhs=codes[:, g, :].bitcast(FP8X4),
+                        rhs_scale=scales[:, g, :],
+                        start=(g == 0),
+                        stop=(g == G - 1),
+                    )
+
+        th = {n: kept("th_" + n, [P, G, J, C], F32) for n in ("mc", "ma", "mu", "mv")}
+        act1 = {n: kept("act1_" + n, [P, G, J, C], F32) for n in ("mc", "ma")}
+        half_of = {"ma": 0, "mc": 1}
+        next_op = {"ma": e1g, "mc": o1g}
+
+        def tanh(key, r0=0, r1=2):
+            m, g, q = key
+            nc.scalar.activation(
+                out=th[m][:, g, 2 * q + r0 : 2 * q + r1, :].rearrange("p j c -> p (j c)"),
+                in_=acc[key][:, r0:r1].rearrange("p j c -> p (j c)"),
+                func=ACT.Tanh,
+            )
+
+        def exp(m, g):
+            t = th[m][:, g].rearrange("p j c -> p (j c)")
+            nc.scalar.activation(out=t, in_=t, func=ACT.Exp)
+
+        def interact(m, g):
+            nc.vector.tensor_tensor(
+                out=act1[m][:, g].rearrange("p j (b d) -> p j b d", b=B),
+                in0=th[m][:, g].rearrange("p j (b d) -> p j b d", b=B),
+                in1=x_t[:, g, :, :, half_of[m], :].rearrange("p b j d -> p j b d"),
+                op=MULT,
+            )
+
+        def gain2(m, g):
+            nc.vector.tensor_tensor(
+                out=next_op[m][0][:, g],
+                in0=act1[m][:, g].rearrange("p j c -> p c j"),
+                in1=g2_t[:, g, :].unsqueeze(1).to_broadcast([P, C, J]),
+                op=MULT,
+            )
+
+        outs = {n: o.rearrange("b (g p j) d -> g p b (j d)", p=P, j=J) for n, o in (("mu", out_0), ("mv", out_1))}
+        base = {"mu": "ma", "mv": "mc"}
+
+        def finish(key, r0=0, r1=2):
+            m, g, q = key
+            j0, j1 = 2 * q + r0, 2 * q + r1
+            res = stage.tile([P, B, r1 - r0, D], F32, name="res", bufs=4)
+            nc.vector.tensor_tensor(
+                out=res[:].rearrange("p b j d -> p j b d"),
+                in0=act1[base[m]][:, g, j0:j1, :].rearrange("p j (b d) -> p j b d", b=B),
+                in1=th[m][:, g, j0:j1, :].rearrange("p j (b d) -> p j b d", b=B),
+                op=(ADD if m == "mu" else SUB),
+            )
+            nc.sync.dma_start(
+                out=outs[m][g, :, :, j0 * D : j1 * D], in_=res[:].rearrange("p b j d -> p b (j d)")
+            )
+
+        for g in range(G):
+            gain1_tensor(eg, 0, g)
+        for g in range(G):
+            quantize_operand(eg, g)
+        widen_at = {}
+        for n in range(8):
+            widen_at[3 + n] = (pairs[12 + n // 2], n % 2)
+        n_pairs = len(pairs)
+        last = pairs[-1]
+        for i in range(n_pairs + 3):
+            if i < n_pairs:
+                transpose(pairs[i])
+                copy_out(pairs[i], "SV" if i == n_pairs - 1 else "SS")
+            if i in (0, 1):
+                gain1_tensor(og, 1, i)
+            if i in (1, 2):
+                quantize_operand(og, i - 1)
+            if i == n_pairs:
+                for r in range(2):
+                    quantize_rows(last, r)
+            elif 1 <= i < n_pairs:
+                quantize_pair(pairs[i - 1])
+            if i in widen_at:
+                widen(*widen_at[i])
+            if i == n_pairs + 1:
+                for r in range(2):
+                    multiply(last, (r,))
+                    acc[last, r] = acc[last]
+            elif 2 <= i < n_pairs + 1:
+                multiply(pairs[i - 2])
+            if i == n_pairs + 2:
+                for r in range(2):
+                    acc[last] = acc[last, r]
+                    tanh(last, r, r + 1)
+                    finish(last, r, r + 1)
+            elif i >= 3:
+                key = pairs[i - 3]
+                m, g, q = key
+                tanh(key)
+                if m in next_op:
+                    if q == 1:
+                        exp(m, g)
+                        interact(m, g)
+                        gain2(m, g)
+                        quantize_operand(next_op[m], g)
+                else:
+                    finish(key)

@@ -20,6 +20,11 @@ G = 2
 J = 4
 C = B * D
 
+ACC_BUFS = 4
+EXTRA = [0,1,2,3,4,5,6,7,8,9,10,11]
+LOADS = [["x",0,0],["x",0,1],["r",0,0],["x",1,0],["x",1,1],["h",0,0],["r",0,1],["p",1],["h",0,1],["p",2],["p",3],["b",1],["p",4],["p",5],["p",6],["p",7],["p",8],["p",9],["p",10],["p",11]]
+STREAM = [["d"],["B",0],["b",0],["B",1],["b",1],["g",0,0],["s",0,0],["T",0],["C",0,0,"S"],["C",0,1,"S"],["W",1],["W",0],["e",0,0],["W",2],["g",0,1],["s",0,1],["T",1],["C",1,0,"S"],["C",1,1,"S"],["e",0,1],["Q",0],["g",1,0],["s",1,0],["T",2],["C",2,0,"S"],["C",2,1,"S"],["Q",1],["W",3],["g",1,1],["s",1,1],["T",3],["C",3,0,"S"],["C",3,1,"S"],["W",4],["Q",2],["e",1,0],["e",1,1],["W",5],["M",0],["H",0],["T",4],["C",4,0,"S"],["C",4,1,"S"],["Q",3],["W",6],["M",1],["H",1],["X","mc",0],["T",5],["C",5,0,"S"],["C",5,1,"V"],["Q",4],["I","mc",0],["M",2],["H",2],["T",6],["C",6,0,"S"],["C",6,1,"S"],["W",7],["Q",5],["M",3],["H",3],["X","mc",1],["T",7],["C",7,0,"S"],["C",7,1,"S"],["G","mc",0],["Q",6],["I","mc",1],["M",4],["H",4],["T",8],["C",8,0,"S"],["C",8,1,"V"],["Q",7],["M",5],["H",5],["X","ma",0],["T",9],["C",9,0,"S"],["C",9,1,"S"],["E","mc",0],["Q",8],["G","mc",1],["I","ma",0],["M",6],["H",6],["T",10],["C",10,0,"V"],["C",10,1,"S"],["E","mc",1],["Q",9],["G","ma",0],["M",7],["H",7],["X","ma",1],["T",11],["C",11,0,"S"],["C",11,1,"S"],["I","ma",1],["Q",10],["M",8],["H",8],["T",12],["C",12,0,"S"],["C",12,1,"S"],["Q",11],["G","ma",1],["M",9],["H",9],["F",8],["T",13],["C",13,0,"S"],["C",13,1,"S"],["Q",12],["E","ma",0],["M",10],["H",10],["F",9],["T",14],["C",14,0,"S"],["C",14,1,"S"],["Q",13],["E","ma",1],["M",11],["H",11],["F",10],["T",15],["C",15,0,"S"],["C",15,1,"S"],["Q",14],["M",12],["H",12],["F",11],["q",15,0],["q",15,1],["M",13],["H",13],["F",12],["M",14],["H",14],["F",13],["m",15,0],["m",15,1],["h",15,0],["h",15,1],["F",14],["f",15,0],["f",15,1]]
+
 FLOPS = 4 * 2 * L * L * C
 
 
@@ -27,9 +32,9 @@ def tile_scinetevenoddinteraction_kernel(tc, x, g1, ma, mc, g2, mu, mv_bytes, mv
     nc = tc.nc
     with ExitStack() as ctx:
         keep = ctx.enter_context(tc.tile_pool(name="keep", bufs=1))
-        stage = ctx.enter_context(tc.tile_pool(name="stage", bufs=3))
+        stage = ctx.enter_context(tc.tile_pool(name="stage", bufs=4))
         tp_pool = ctx.enter_context(tc.psum_pool(name="tp", bufs=4))
-        acc_pool = ctx.enter_context(tc.psum_pool(name="acc", bufs=4))
+        acc_pool = ctx.enter_context(tc.psum_pool(name="acc", bufs=ACC_BUFS))
 
         def kept(name, shape, dtype):
             return keep.tile(shape, dtype, name=name, align_bytes=64)
@@ -38,6 +43,8 @@ def tile_scinetevenoddinteraction_kernel(tc, x, g1, ma, mc, g2, mu, mv_bytes, mv
         g2_t = kept("g2_t", [P, G, J], BF16)
         nc.scalar.dma_start(out=g1_t[:], in_=g1.rearrange("(g p j) -> p g j", p=P, j=J))
         nc.scalar.dma_start(out=g2_t[:], in_=g2.rearrange("(g p j) -> p g j", p=P, j=J))
+        sc = kept("sc", [P, 8], F32)
+        nc.scalar.dma_start(out=sc[:], in_=mv_scale.rearrange("o (p n) -> p (o n)", p=P))
         warm = kept("warm", [P, 1], F32)
         nc.gpsimd.memset(warm[:], 0.0)
         nc.scalar.activation(out=warm[:], in_=warm[:], func=ACT.Tanh)
@@ -46,12 +53,6 @@ def tile_scinetevenoddinteraction_kernel(tc, x, g1, ma, mc, g2, mu, mv_bytes, mv
         ident_bf = kept("ident_bf", [P, P], BF16)
         make_identity(nc, ident_bf[:])
         diag = kept("diag", [P, G, J, P], BF16)
-        nc.vector.tensor_tensor(
-            out=diag[:].rearrange("p g j i -> p (g j) i"),
-            in0=ident_bf[:].unsqueeze(1).to_broadcast([P, G * J, P]),
-            in1=g1_t[:].rearrange("p g j -> p (g j)").unsqueeze(2).to_broadcast([P, G * J, P]),
-            op=MULT,
-        )
 
         x_t = kept("x_t", [P, G, B, J, 2, D], BF16)
         x_v = x.rearrange("b (g p j) h d -> g b p (j h d)", p=P, j=J)
@@ -70,18 +71,32 @@ def tile_scinetevenoddinteraction_kernel(tc, x, g1, ma, mc, g2, mu, mv_bytes, mv
 
         mvb = kept("mvb", [P, G, J, L], U8)
         mvs = kept("mvs", [P, L], F32)
-        key = pairs[0]
-        for g in range(G):
-            for b in range(B):
-                load_x(g, b)
-            nc.sync.dma_start(out=raw[key][:, g, :], in_=views["mc"][0, :, g, :])
-        for key in pairs[1:6]:
-            load_pair(key)
-        nc.sync.dma_start(out=mvs[:], in_=mv_scale.rearrange("o k -> (o k)").partition_broadcast(P))
-        for g in range(G):
-            nc.sync.dma_start(out=mvb[:, g].rearrange("p j k -> p (j k)"), in_=mv_bytes.rearrange("(g p j) k -> g p (j k)", p=P, j=J)[g])
-        for key in pairs[6:12]:
-            load_pair(key)
+        def load_row(key, r):
+            m, g, q = key
+            nc.sync.dma_start(out=raw[key][:, r, :], in_=views[m][g, :, 2 * q + r, :])
+
+
+        def load_bytes(g):
+            nc.sync.dma_start(
+                out=mvb[:, g].rearrange("p j k -> p (j k)"),
+                in_=mv_bytes.rearrange("(g p j) k -> g p (j k)", p=P, j=J)[g],
+            )
+
+        for n in LOADS:
+            if n[0] == "x":
+                load_x(n[1], n[2])
+            elif n[0] == "r":
+                load_row(pairs[n[1]], n[2])
+            elif n[0] == "h":
+                g, q = n[1], n[2]
+                nc.sync.dma_start(
+                    out=mvb[:, g, 2 * q : 2 * q + 2].rearrange("p j k -> p (j k)"),
+                    in_=mv_bytes.rearrange("(g p j) k -> g p j k", p=P, j=J)[g, :, 2 * q : 2 * q + 2].rearrange("p j k -> p (j k)"),
+                )
+            elif n[0] == "p":
+                load_pair(pairs[n[1]])
+            else:
+                load_bytes(n[1])
 
         def operand(name):
             return (
@@ -98,8 +113,22 @@ def tile_scinetevenoddinteraction_kernel(tc, x, g1, ma, mc, g2, mu, mv_bytes, mv
                 out=codes[:, g, :].bitcast(FP8X4), scales=scales[:, g, :], in_=inter[:, g].rearrange("p c j -> p (c j)")
             )
 
+        gain_banks = {}
+
+        def build_diag():
+            g1_cols = g1_t[:].rearrange("p g j -> p (g j)")
+            for n in range(G * J):
+                nc.vector.tensor_scalar(
+                    out=diag[:].rearrange("p g j i -> p (g j) i")[:, n, :],
+                    in0=ident_bf[:],
+                    scalar1=g1_cols[:, n : n + 1],
+                    scalar2=None,
+                    op0=MULT,
+                )
+
         def gain1_tensor(op, half, g):
             bank = acc_pool.tile([P, J, C], BF16, name="gain_bank", tag="acc")
+            gain_banks[half, g] = bank
             for j in range(J):
                 nc.tensor.matmul(
                     out=bank[:, j, :].rearrange("p (b d) -> p b d", b=B),
@@ -108,7 +137,17 @@ def tile_scinetevenoddinteraction_kernel(tc, x, g1, ma, mc, g2, mu, mv_bytes, mv
                     start=True,
                     stop=True,
                 )
-            nc.scalar.copy(out=op[0][:, g], in_=bank[:].rearrange("p j c -> p c j"))
+
+        def gain1_exit(op, half, g):
+            nc.scalar.copy(out=op[0][:, g], in_=gain_banks[half, g][:].rearrange("p j c -> p c j"))
+
+        def gain1_vector(op, half, g):
+            nc.vector.tensor_tensor(
+                out=op[0][:, g].rearrange("p (b d) j -> p b d j", b=B),
+                in0=x_t[:, g, :, :, half, :].rearrange("p b j d -> p b d j"),
+                in1=g1_t[:, g, :].unsqueeze(1).unsqueeze(1).to_broadcast([P, B, D, J]),
+                op=MULT,
+            )
 
         w_t, w_c, w_s, tp, acc = {}, {}, {}, {}, {}
 
@@ -128,21 +167,21 @@ def tile_scinetevenoddinteraction_kernel(tc, x, g1, ma, mc, g2, mu, mv_bytes, mv
                         k0 = 512 * r + 256 * g
                         nc.tensor.transpose(bank[:, g, u, :], words[:, k0 + u : k0 + 256 : 2], ident[:])
 
-        def copy_out(key, engines):
-            w_t[key] = stage.tile([P, 2, G, P, J], BF16, name="w_t", align_bytes=64)
+        def copy_out(key, r, engine):
+            if key not in w_t:
+                w_t[key] = stage.tile([P, 2, G, P, J], BF16, name="w_t", align_bytes=64, bufs=4)
             words = w_t[key][:].rearrange("p r g c j -> p (r g c j)").bitcast(F32)
-            for r in range(2):
-                o = words[:, 512 * r : 512 * (r + 1)].rearrange("p (g c u) -> p g c u", g=G, u=2)
-                i = tp[key, r][:].rearrange("p g u c -> p g c u")
-                if engines[r] == "S":
-                    nc.scalar.copy(out=o, in_=i)
-                else:
-                    nc.vector.tensor_copy(out=o, in_=i)
+            o = words[:, 512 * r : 512 * (r + 1)].rearrange("p (g c u) -> p g c u", g=G, u=2)
+            i = tp[key, r][:].rearrange("p g u c -> p g c u")
+            if engine == "S":
+                nc.scalar.copy(out=o, in_=i)
+            else:
+                nc.vector.tensor_copy(out=o, in_=i)
 
         def quantize_rows(key, r):
             if r == 0:
-                w_c[key] = stage.tile([P, 2 * G * P], U32, name="w_c", align_bytes=64, bufs=5)
-                w_s[key] = stage.tile([P, 2 * G * P], U8, name="w_s", align_bytes=64, bufs=5)
+                w_c[key] = stage.tile([P, 2 * G * P], U32, name="w_c", align_bytes=64, bufs=6)
+                w_s[key] = stage.tile([P, 2 * G * P], U8, name="w_s", align_bytes=64, bufs=6)
             c0 = r * G * P
             nc.vector.quantize_mx(
                 out=w_c[key][:, c0 : c0 + G * P].bitcast(FP8X4),
@@ -151,8 +190,8 @@ def tile_scinetevenoddinteraction_kernel(tc, x, g1, ma, mc, g2, mu, mv_bytes, mv
             )
 
         def quantize_pair(key):
-            w_c[key] = stage.tile([P, 2 * G * P], U32, name="w_c", align_bytes=64, bufs=5)
-            w_s[key] = stage.tile([P, 2 * G * P], U8, name="w_s", align_bytes=64, bufs=5)
+            w_c[key] = stage.tile([P, 2 * G * P], U32, name="w_c", align_bytes=64, bufs=6)
+            w_s[key] = stage.tile([P, 2 * G * P], U8, name="w_s", align_bytes=64, bufs=6)
             nc.vector.quantize_mx(
                 out=w_c[key][:].bitcast(FP8X4), scales=w_s[key][:], in_=w_t[key][:].rearrange("p r g c j -> p (r g c j)")
             )
@@ -162,8 +201,10 @@ def tile_scinetevenoddinteraction_kernel(tc, x, g1, ma, mc, g2, mu, mv_bytes, mv
         def multiply(key, rows=(0, 1)):
             codes, scales = rhs_of[key[0]][1:]
             acc[key] = acc_pool.tile([P, 2, C], F32, name="acc_bank", tag="acc")
+            extra = 1 if pairs.index(key) in EXTRA else 0
             for r in rows:
-                for g in range(G):
+                passes = [(0, True, True)] * (extra if r == 0 else 0) + [(g, g == 0, g == G - 1) for g in range(G)]
+                for g, first, final in passes:
                     c0 = (r * G + g) * P
                     nc.tensor.matmul_mx(
                         out=acc[key][:, r, :],
@@ -171,8 +212,8 @@ def tile_scinetevenoddinteraction_kernel(tc, x, g1, ma, mc, g2, mu, mv_bytes, mv
                         lhsT_scale=w_s[key][:, c0 : c0 + P],
                         rhs=codes[:, g, :].bitcast(FP8X4),
                         rhs_scale=scales[:, g, :],
-                        start=(g == 0),
-                        stop=(g == G - 1),
+                        start=first,
+                        stop=final,
                     )
 
         th = {n: kept("th_" + n, [P, G, J, C], F32) for n in ("mc", "ma", "mu", "mv")}
@@ -225,50 +266,73 @@ def tile_scinetevenoddinteraction_kernel(tc, x, g1, ma, mc, g2, mu, mv_bytes, mv
                 out=outs[m][g, :, :, j0 * D : j1 * D], in_=res[:].rearrange("p b j d -> p b (j d)")
             )
 
-        for g in range(G):
-            gain1_tensor(eg, 0, g)
-        for g in range(G):
-            quantize_operand(eg, g)
-        widen_at = {}
-        for n in range(8):
-            widen_at[3 + n] = (pairs[12 + n // 2], n % 2)
         n_pairs = len(pairs)
         last = pairs[-1]
-        for i in range(n_pairs + 3):
-            if i < n_pairs:
-                transpose(pairs[i])
-                copy_out(pairs[i], "SV" if i == n_pairs - 1 else "SS")
-            if i in (0, 1):
-                gain1_tensor(og, 1, i)
-            if i in (1, 2):
-                quantize_operand(og, i - 1)
-            if i == n_pairs:
-                for r in range(2):
-                    quantize_rows(last, r)
-            elif 1 <= i < n_pairs:
-                quantize_pair(pairs[i - 1])
-            if i in widen_at:
-                widen(*widen_at[i])
-            if i == n_pairs + 1:
-                for r in range(2):
-                    multiply(last, (r,))
-                    acc[last, r] = acc[last]
-            elif 2 <= i < n_pairs + 1:
-                multiply(pairs[i - 2])
-            if i == n_pairs + 2:
-                for r in range(2):
-                    acc[last] = acc[last, r]
-                    tanh(last, r, r + 1)
-                    finish(last, r, r + 1)
-            elif i >= 3:
-                key = pairs[i - 3]
-                m, g, q = key
-                tanh(key)
-                if m in next_op:
-                    if q == 1:
-                        exp(m, g)
-                        interact(m, g)
-                        gain2(m, g)
-                        quantize_operand(next_op[m], g)
-                else:
-                    finish(key)
+        scratch = {}
+
+        banks = {}
+
+        def spread_scale(h):
+            bank = acc_pool.tile([P, 4, P], F32, name="scale_bank", tag="acc")
+            banks["scale", h] = bank
+            for n in range(4):
+                nc.tensor.transpose(bank[:, n, :], sc[:, 4 * h + n : 4 * h + n + 1].to_broadcast([P, P]), ident[:])
+
+        def spread_exit(h):
+            nc.scalar.copy(
+                out=mvs[:].rearrange("p (k n) -> p k n", n=8)[:, :, 4 * h : 4 * h + 4],
+                in_=banks["scale", h][:].rearrange("p n k -> p k n"),
+            )
+
+        def do(item):
+            k = item[0]
+            if k == "T":
+                transpose(pairs[item[1]])
+            elif k == "C":
+                copy_out(pairs[item[1]], item[2], item[3])
+            elif k == "Q":
+                quantize_pair(pairs[item[1]])
+            elif k == "q":
+                quantize_rows(pairs[item[1]], item[2])
+            elif k == "M":
+                multiply(pairs[item[1]])
+            elif k == "m":
+                multiply(pairs[item[1]], (item[2],))
+                acc[pairs[item[1]], item[2]] = acc[pairs[item[1]]]
+            elif k == "H":
+                tanh(pairs[item[1]])
+            elif k == "h":
+                acc[pairs[item[1]]] = acc[pairs[item[1]], item[2]]
+                tanh(pairs[item[1]], item[2], item[2] + 1)
+            elif k == "F":
+                finish(pairs[item[1]])
+            elif k == "f":
+                finish(pairs[item[1]], item[2], item[2] + 1)
+            elif k == "X":
+                exp(item[1], item[2])
+            elif k == "I":
+                interact(item[1], item[2])
+            elif k == "G":
+                gain2(item[1], item[2])
+            elif k == "E":
+                quantize_operand(next_op[item[1]], item[2])
+            elif k == "W":
+                widen(pairs[12 + item[1] // 2], item[1] % 2)
+            elif k == "g":
+                gain1_tensor((eg, og)[item[1]], item[1], item[2])
+            elif k == "d":
+                build_diag()
+            elif k == "v":
+                gain1_vector((eg, og)[item[1]], item[1], item[2])
+            elif k == "e":
+                quantize_operand((eg, og)[item[1]], item[2])
+            elif k == "B":
+                spread_scale(item[1])
+            elif k == "b":
+                spread_exit(item[1])
+            elif k == "s":
+                gain1_exit((eg, og)[item[1]], item[1], item[2])
+
+        with tc.manual_schedule():
+            for item in STREAM:
+                do(item)

@@ -23,7 +23,7 @@ C = B * D
 ACC_BUFS = 4
 EXTRA = [0,1,2,3,4,5,6,7,8,9,10,11]
 LOADS = [["x",0,0],["x",0,1],["r",0,0],["x",1,0],["x",1,1],["h",0,0],["r",0,1],["p",1],["h",0,1],["p",2],["p",3],["b",1],["p",4],["p",5],["p",6],["p",7],["p",8],["p",9],["p",10],["p",11]]
-STREAM = [["d"],["B",0],["b",0],["B",1],["b",1],["g",0,0],["s",0,0],["T",0],["C",0,0,"S"],["C",0,1,"S"],["W",1],["W",0],["e",0,0],["W",2],["g",0,1],["s",0,1],["T",1],["C",1,0,"S"],["C",1,1,"S"],["e",0,1],["Q",0],["g",1,0],["s",1,0],["T",2],["C",2,0,"S"],["C",2,1,"S"],["Q",1],["W",3],["g",1,1],["s",1,1],["T",3],["C",3,0,"S"],["C",3,1,"S"],["W",4],["Q",2],["e",1,0],["e",1,1],["W",5],["M",0],["H",0],["T",4],["C",4,0,"S"],["C",4,1,"S"],["Q",3],["W",6],["M",1],["H",1],["X","mc",0],["T",5],["C",5,0,"S"],["C",5,1,"V"],["Q",4],["I","mc",0],["M",2],["H",2],["T",6],["C",6,0,"S"],["C",6,1,"S"],["W",7],["Q",5],["M",3],["H",3],["X","mc",1],["T",7],["C",7,0,"S"],["C",7,1,"S"],["G","mc",0],["Q",6],["I","mc",1],["M",4],["H",4],["T",8],["C",8,0,"S"],["C",8,1,"V"],["Q",7],["M",5],["H",5],["X","ma",0],["T",9],["C",9,0,"S"],["C",9,1,"S"],["E","mc",0],["Q",8],["G","mc",1],["I","ma",0],["M",6],["H",6],["T",10],["C",10,0,"V"],["C",10,1,"S"],["E","mc",1],["Q",9],["G","ma",0],["M",7],["H",7],["X","ma",1],["T",11],["C",11,0,"S"],["C",11,1,"S"],["I","ma",1],["Q",10],["M",8],["H",8],["T",12],["C",12,0,"S"],["C",12,1,"S"],["Q",11],["G","ma",1],["M",9],["H",9],["F",8],["T",13],["C",13,0,"S"],["C",13,1,"S"],["Q",12],["E","ma",0],["M",10],["H",10],["F",9],["T",14],["C",14,0,"S"],["C",14,1,"S"],["Q",13],["E","ma",1],["M",11],["H",11],["F",10],["T",15],["C",15,0,"S"],["C",15,1,"S"],["Q",14],["M",12],["H",12],["F",11],["q",15,0],["q",15,1],["M",13],["H",13],["F",12],["M",14],["H",14],["F",13],["m",15,0],["m",15,1],["h",15,0],["h",15,1],["F",14],["f",15,0],["f",15,1]]
+STREAM = [["d"],["B",0],["b",0],["B",1],["b",1],["g",0,0],["s",0,0],["T",0],["C",0,0,"S"],["C",0,1,"S"],["W",0],["W",1],["W",2],["g",0,1],["s",0,1],["T",1],["C",1,0,"S"],["C",1,1,"S"],["W",3],["Q",0],["g",1,0],["s",1,0],["T",2],["C",2,0,"S"],["C",2,1,"S"],["Q",1],["e",0],["g",1,1],["s",1,1],["T",3],["C",3,0,"S"],["C",3,1,"S"],["Q",2],["M",0],["H",0],["T",4],["C",4,0,"S"],["C",4,1,"S"],["W",4],["Q",3],["e",1],["W",5],["M",1],["H",1],["X","mc",0],["T",5],["C",5,0,"S"],["C",5,1,"S"],["Q",4],["W",6],["M",2],["H",2],["T",6],["C",6,0,"S"],["C",6,1,"S"],["W",7],["I","mc",0],["Q",5],["G","mc",0],["M",3],["H",3],["X","mc",1],["T",7],["C",7,0,"V"],["C",7,1,"S"],["Q",6],["M",4],["H",4],["T",8],["C",8,0,"V"],["C",8,1,"S"],["Q",7],["I","mc",1],["M",5],["H",5],["X","ma",0],["T",9],["C",9,0,"S"],["C",9,1,"S"],["Q",8],["G","mc",1],["M",6],["H",6],["T",10],["C",10,0,"V"],["C",10,1,"S"],["E","mc"],["Q",9],["M",7],["H",7],["X","ma",1],["T",11],["C",11,0,"S"],["C",11,1,"S"],["I","ma",0],["Q",10],["G","ma",0],["I","ma",1],["M",8],["H",8],["T",12],["C",12,0,"S"],["C",12,1,"S"],["Q",11],["M",9],["H",9],["T",13],["C",13,0,"S"],["C",13,1,"S"],["G","ma",1],["Q",12],["E","ma"],["M",10],["H",10],["F",8],["T",14],["C",14,0,"S"],["C",14,1,"S"],["Q",13],["M",11],["H",11],["T",15],["C",15,0,"S"],["C",15,1,"S"],["Q",14],["M",12],["H",12],["F",10],["q",15,0],["q",15,1],["M",13],["H",13],["M",14],["H",14],["F",12],["m",15,0],["m",15,1],["h",15,0],["h",15,1],["F",14],["f",15,0],["f",15,1]]
 
 FLOPS = 4 * 2 * L * L * C
 
@@ -107,10 +107,12 @@ def tile_scinetevenoddinteraction_kernel(tc, x, g1, ma, mc, g2, mu, mv_bytes, mv
 
         eg, og, e1g, o1g = operand("eg"), operand("og"), operand("e1g"), operand("o1g")
 
-        def quantize_operand(op, g):
+        def quantize_operand(op):
             inter, codes, scales = op
             nc.vector.quantize_mx(
-                out=codes[:, g, :].bitcast(FP8X4), scales=scales[:, g, :], in_=inter[:, g].rearrange("p c j -> p (c j)")
+                out=codes[:].rearrange("p g c -> p (g c)").bitcast(FP8X4),
+                scales=scales[:].rearrange("p g c -> p (g c)"),
+                in_=inter[:].rearrange("p g c j -> p (g c j)"),
             )
 
         gain_banks = {}
@@ -243,9 +245,9 @@ def tile_scinetevenoddinteraction_kernel(tc, x, g1, ma, mc, g2, mu, mv_bytes, mv
 
         def gain2(m, g):
             nc.vector.tensor_tensor(
-                out=next_op[m][0][:, g],
-                in0=act1[m][:, g].rearrange("p j c -> p c j"),
-                in1=g2_t[:, g, :].unsqueeze(1).to_broadcast([P, C, J]),
+                out=next_op[m][0][:, g].rearrange("p (c i) j -> p c j i", i=4),
+                in0=act1[m][:, g].rearrange("p j (c i) -> p c j i", i=4),
+                in1=g2_t[:, g, :].unsqueeze(1).unsqueeze(3).to_broadcast([P, C // 4, J, 4]),
                 op=MULT,
             )
 
@@ -305,7 +307,7 @@ def tile_scinetevenoddinteraction_kernel(tc, x, g1, ma, mc, g2, mu, mv_bytes, mv
                 acc[pairs[item[1]]] = acc[pairs[item[1]], item[2]]
                 tanh(pairs[item[1]], item[2], item[2] + 1)
             elif k == "F":
-                finish(pairs[item[1]])
+                finish(pairs[item[1]], 0, 4 if item[1] < 14 else 2)
             elif k == "f":
                 finish(pairs[item[1]], item[2], item[2] + 1)
             elif k == "X":
@@ -315,7 +317,7 @@ def tile_scinetevenoddinteraction_kernel(tc, x, g1, ma, mc, g2, mu, mv_bytes, mv
             elif k == "G":
                 gain2(item[1], item[2])
             elif k == "E":
-                quantize_operand(next_op[item[1]], item[2])
+                quantize_operand(next_op[item[1]])
             elif k == "W":
                 widen(pairs[12 + item[1] // 2], item[1] % 2)
             elif k == "g":
@@ -325,7 +327,7 @@ def tile_scinetevenoddinteraction_kernel(tc, x, g1, ma, mc, g2, mu, mv_bytes, mv
             elif k == "v":
                 gain1_vector((eg, og)[item[1]], item[1], item[2])
             elif k == "e":
-                quantize_operand((eg, og)[item[1]], item[2])
+                quantize_operand((eg, og)[item[1]])
             elif k == "B":
                 spread_scale(item[1])
             elif k == "b":

@@ -21,9 +21,9 @@ J = 4
 C = B * D
 
 ACC_BUFS = 4
-EXTRA = [0,1,2,3,4,5,6,7,8,9,10,11]
-LOADS = [["x",0,0],["x",0,1],["r",0,0],["x",1,0],["x",1,1],["h",0,0],["r",0,1],["p",1],["h",0,1],["p",2],["p",3],["b",1],["p",4],["p",5],["p",6],["p",7],["p",8],["p",9],["p",10],["p",11]]
-STREAM = [["d"],["B",0],["b",0],["B",1],["b",1],["g",0,0],["s",0,0],["T",0],["C",0,0,"S"],["C",0,1,"S"],["W",0],["W",1],["W",2],["g",0,1],["s",0,1],["T",1],["C",1,0,"S"],["C",1,1,"S"],["W",3],["Q",0],["g",1,0],["s",1,0],["T",2],["C",2,0,"S"],["C",2,1,"S"],["Q",1],["e",0],["g",1,1],["s",1,1],["T",3],["C",3,0,"S"],["C",3,1,"S"],["Q",2],["M",0],["H",0],["T",4],["C",4,0,"S"],["C",4,1,"S"],["W",4],["Q",3],["e",1],["W",5],["M",1],["H",1],["X","mc",0],["T",5],["C",5,0,"S"],["C",5,1,"S"],["Q",4],["W",6],["M",2],["H",2],["T",6],["C",6,0,"S"],["C",6,1,"S"],["W",7],["I","mc",0],["Q",5],["G","mc",0],["M",3],["H",3],["X","mc",1],["T",7],["C",7,0,"V"],["C",7,1,"S"],["Q",6],["M",4],["H",4],["T",8],["C",8,0,"V"],["C",8,1,"S"],["Q",7],["I","mc",1],["M",5],["H",5],["X","ma",0],["T",9],["C",9,0,"S"],["C",9,1,"S"],["Q",8],["G","mc",1],["M",6],["H",6],["T",10],["C",10,0,"V"],["C",10,1,"S"],["E","mc"],["Q",9],["M",7],["H",7],["X","ma",1],["T",11],["C",11,0,"S"],["C",11,1,"S"],["I","ma",0],["Q",10],["G","ma",0],["I","ma",1],["M",8],["H",8],["T",12],["C",12,0,"S"],["C",12,1,"S"],["Q",11],["M",9],["H",9],["T",13],["C",13,0,"S"],["C",13,1,"S"],["G","ma",1],["Q",12],["E","ma"],["M",10],["H",10],["F",8],["T",14],["C",14,0,"S"],["C",14,1,"S"],["Q",13],["M",11],["H",11],["T",15],["C",15,0,"S"],["C",15,1,"S"],["Q",14],["M",12],["H",12],["F",10],["q",15,0],["q",15,1],["M",13],["H",13],["M",14],["H",14],["F",12],["m",15,0],["m",15,1],["h",15,0],["h",15,1],["F",14],["f",15,0],["f",15,1]]
+EXTRA = [0,1,2,3,4,5,6,7]
+LOADS = [["x",0,0],["x",0,1],["x",1,0],["x",1,1],["h",0,0],["r",0,0],["r",0,1],["p",1],["h",0,1],["p",2],["p",3],["b",1],["p",4],["p",5],["p",6],["p",7],["p",8],["p",9],["p",10],["p",11]]
+STREAM = [["d"],["D"],["B",0],["b",0],["B",1],["b",1],["g",0,0],["s",0,0],["g",0,1],["s",0,1],["T",0],["C",0,0,"S"],["C",0,1,"S"],["W",0],["W",1],["e",0],["g",1,0],["s",1,0],["T",1],["C",1,0,"S"],["C",1,1,"S"],["W",2],["Q",0],["W",3],["g",1,1],["s",1,1],["T",2],["C",2,0,"S"],["C",2,1,"S"],["Q",1],["W",4],["M",0],["H",0],["T",3],["C",3,0,"S"],["C",3,1,"S"],["W",5],["Q",2],["e",1],["M",1],["H",1],["X","mc",0],["T",4],["C",4,0,"S"],["C",4,1,"S"],["W",6],["Q",3],["W",7],["M",2],["H",2],["T",5],["C",5,0,"S"],["C",5,1,"V"],["Q",4],["M",3],["H",3],["X","mc",1],["T",6],["C",6,0,"V"],["C",6,1,"S"],["Q",5],["I","mc",0],["M",4],["H",4],["T",7],["C",7,0,"S"],["C",7,1,"S"],["Q",6],["I","mc",1],["M",5],["H",5],["X","ma",0],["T",8],["C",8,0,"S"],["C",8,1,"S"],["G","mc",0],["Q",7],["M",6],["H",6],["T",9],["C",9,0,"S"],["C",9,1,"S"],["G","mc",1],["E","mc"],["Q",8],["M",7],["H",7],["X","ma",1],["T",10],["C",10,0,"V"],["C",10,1,"S"],["Q",9],["I","ma",0],["T",11],["C",11,0,"S"],["C",11,1,"S"],["I","ma",1],["Q",10],["G","ma",0],["M",8],["T",12],["C",12,0,"S"],["C",12,1,"S"],["G","ma",1],["Q",11],["M",9],["H",8],["T",13],["C",13,0,"S"],["C",13,1,"S"],["Q",12],["E","ma"],["M",10],["H",9],["T",14],["C",14,0,"S"],["C",14,1,"S"],["Q",13],["M",11],["H",10],["F",8],["T",15],["C",15,0,"S"],["C",15,1,"S"],["Q",14],["M",12],["H",11],["q",15,0],["q",15,1],["M",13],["H",12],["F",10],["M",14],["H",13],["m",15,0],["m",15,1],["H",14],["F",12],["h",15,0],["h",15,1],["F",14],["f",15,0],["f",15,1]]
 
 FLOPS = 4 * 2 * L * L * C
 
@@ -41,10 +41,12 @@ def tile_scinetevenoddinteraction_kernel(tc, x, g1, ma, mc, g2, mu, mv_bytes, mv
 
         g1_t = kept("g1_t", [P, G, J], BF16)
         g2_t = kept("g2_t", [P, G, J], BF16)
-        nc.scalar.dma_start(out=g1_t[:], in_=g1.rearrange("(g p j) -> p g j", p=P, j=J))
-        nc.scalar.dma_start(out=g2_t[:], in_=g2.rearrange("(g p j) -> p g j", p=P, j=J))
         sc = kept("sc", [P, 8], F32)
         nc.scalar.dma_start(out=sc[:], in_=mv_scale.rearrange("o (p n) -> p (o n)", p=P))
+        nc.scalar.dma_start(out=g1_t[:], in_=g1.rearrange("(g p j) -> p g j", p=P, j=J))
+        nc.scalar.dma_start(out=g2_t[:], in_=g2.rearrange("(g p j) -> p g j", p=P, j=J))
+        zeros = kept("zeros", [P, 512], BF16)
+        nc.vector.memset(zeros[:], 0.0)
         warm = kept("warm", [P, 1], F32)
         nc.gpsimd.memset(warm[:], 0.0)
         nc.scalar.activation(out=warm[:], in_=warm[:], func=ACT.Tanh)
@@ -274,6 +276,11 @@ def tile_scinetevenoddinteraction_kernel(tc, x, g1, ma, mc, g2, mu, mv_bytes, mv
 
         banks = {}
 
+        def warm_up():
+            bank = acc_pool.tile([P, 512], F32, name="warm_bank", tag="acc")
+            for n in range(4):
+                nc.tensor.matmul(out=bank[:], lhsT=zeros[:, :P], rhs=zeros[:], start=True, stop=True)
+
         def spread_scale(h):
             bank = acc_pool.tile([P, 4, P], F32, name="scale_bank", tag="acc")
             banks["scale", h] = bank
@@ -328,6 +335,8 @@ def tile_scinetevenoddinteraction_kernel(tc, x, g1, ma, mc, g2, mu, mv_bytes, mv
                 gain1_vector((eg, og)[item[1]], item[1], item[2])
             elif k == "e":
                 quantize_operand((eg, og)[item[1]])
+            elif k == "D":
+                warm_up()
             elif k == "B":
                 spread_scale(item[1])
             elif k == "b":

from contextlib import ExitStack

import concourse.mybir as mybir
from concourse.masks import make_identity

F32 = mybir.dt.float32
BF16 = mybir.dt.bfloat16
U32 = mybir.dt.uint32
U8 = mybir.dt.uint8
FP8 = mybir.dt.float8_e4m3fn
FP8X4 = mybir.dt.float8_e4m3fn_x4
ACT = mybir.ActivationFunctionType
MULT = mybir.AluOpType.mult
ADD = mybir.AluOpType.add
SUB = mybir.AluOpType.subtract

P = 128
B, L, D = 2, 1024, 128
G = 2
J = 4
C = B * D

ACC_BUFS = 4
EXTRA = [0,1,2,3,4,5,6,7]
LOADS = [["x",0,0],["x",0,1],["x",1,0],["x",1,1],["h",0,0],["r",0,0],["r",0,1],["p",1],["h",0,1],["p",2],["p",3],["b",1],["p",4],["p",5],["p",6],["p",7],["p",8],["p",9],["p",10],["p",11]]
STREAM = [["d"],["D"],["B",0],["b",0],["B",1],["b",1],["g",0,0],["s",0,0],["g",0,1],["s",0,1],["T",0],["C",0,0,"S"],["C",0,1,"S"],["W",0],["W",1],["e",0],["g",1,0],["s",1,0],["T",1],["C",1,0,"S"],["C",1,1,"S"],["W",2],["Q",0],["W",3],["g",1,1],["s",1,1],["T",2],["C",2,0,"S"],["C",2,1,"S"],["Q",1],["W",4],["M",0],["H",0],["T",3],["C",3,0,"S"],["C",3,1,"S"],["W",5],["Q",2],["e",1],["M",1],["H",1],["X","mc",0],["T",4],["C",4,0,"S"],["C",4,1,"S"],["W",6],["Q",3],["W",7],["M",2],["H",2],["T",5],["C",5,0,"S"],["C",5,1,"V"],["Q",4],["M",3],["H",3],["X","mc",1],["T",6],["C",6,0,"V"],["C",6,1,"S"],["Q",5],["I","mc",0],["M",4],["H",4],["T",7],["C",7,0,"S"],["C",7,1,"S"],["Q",6],["I","mc",1],["M",5],["H",5],["X","ma",0],["T",8],["C",8,0,"S"],["C",8,1,"S"],["G","mc",0],["Q",7],["M",6],["H",6],["T",9],["C",9,0,"S"],["C",9,1,"S"],["G","mc",1],["E","mc"],["Q",8],["M",7],["H",7],["X","ma",1],["T",10],["C",10,0,"V"],["C",10,1,"S"],["Q",9],["I","ma",0],["T",11],["C",11,0,"S"],["C",11,1,"S"],["I","ma",1],["Q",10],["G","ma",0],["M",8],["T",12],["C",12,0,"S"],["C",12,1,"S"],["G","ma",1],["Q",11],["M",9],["H",8],["T",13],["C",13,0,"S"],["C",13,1,"S"],["Q",12],["E","ma"],["M",10],["H",9],["T",14],["C",14,0,"S"],["C",14,1,"S"],["Q",13],["M",11],["H",10],["F",8],["T",15],["C",15,0,"S"],["C",15,1,"S"],["Q",14],["M",12],["H",11],["q",15,0],["q",15,1],["M",13],["H",12],["F",10],["M",14],["H",13],["m",15,0],["m",15,1],["H",14],["F",12],["h",15,0],["h",15,1],["F",14],["f",15,0],["f",15,1]]

FLOPS = 4 * 2 * L * L * C


def tile_scinetevenoddinteraction_kernel(tc, x, g1, ma, mc, g2, mu, mv_bytes, mv_scale, out_0, out_1):
    nc = tc.nc
    with ExitStack() as ctx:
        keep = ctx.enter_context(tc.tile_pool(name="keep", bufs=1))
        stage = ctx.enter_context(tc.tile_pool(name="stage", bufs=4))
        tp_pool = ctx.enter_context(tc.psum_pool(name="tp", bufs=4))
        acc_pool = ctx.enter_context(tc.psum_pool(name="acc", bufs=ACC_BUFS))

        def kept(name, shape, dtype):
            return keep.tile(shape, dtype, name=name, align_bytes=64)

        g1_t = kept("g1_t", [P, G, J], BF16)
        g2_t = kept("g2_t", [P, G, J], BF16)
        sc = kept("sc", [P, 8], F32)
        nc.scalar.dma_start(out=sc[:], in_=mv_scale.rearrange("o (p n) -> p (o n)", p=P))
        nc.scalar.dma_start(out=g1_t[:], in_=g1.rearrange("(g p j) -> p g j", p=P, j=J))
        nc.scalar.dma_start(out=g2_t[:], in_=g2.rearrange("(g p j) -> p g j", p=P, j=J))
        zeros = kept("zeros", [P, 512], BF16)
        nc.vector.memset(zeros[:], 0.0)
        warm = kept("warm", [P, 1], F32)
        nc.gpsimd.memset(warm[:], 0.0)
        nc.scalar.activation(out=warm[:], in_=warm[:], func=ACT.Tanh)
        ident = kept("ident", [P, P], F32)
        make_identity(nc, ident[:])
        ident_bf = kept("ident_bf", [P, P], BF16)
        make_identity(nc, ident_bf[:])
        diag = kept("diag", [P, G, J, P], BF16)

        x_t = kept("x_t", [P, G, B, J, 2, D], BF16)
        x_v = x.rearrange("b (g p j) h d -> g b p (j h d)", p=P, j=J)
        raw = {}
        pairs = [(m, g, q) for m in ("mc", "ma", "mu", "mv") for g in range(G) for q in range(2)]
        for key in pairs:
            raw[key] = kept("raw_%s_%d_%d" % key, [P, 2, L], BF16)
        views = {n: a.rearrange("(g p j) k -> g p j k", p=P, j=J) for n, a in (("mc", mc), ("ma", ma), ("mu", mu))}

        def load_pair(key):
            m, g, q = key
            nc.sync.dma_start(out=raw[key][:], in_=views[m][g, :, 2 * q : 2 * q + 2, :])

        def load_x(g, b):
            nc.sync.dma_start(out=x_t[:, g, b].rearrange("p j h d -> p (j h d)"), in_=x_v[g, b])

        mvb = kept("mvb", [P, G, J, L], U8)
        mvs = kept("mvs", [P, L], F32)
        def load_row(key, r):
            m, g, q = key
            nc.sync.dma_start(out=raw[key][:, r, :], in_=views[m][g, :, 2 * q + r, :])


        def load_bytes(g):
            nc.sync.dma_start(
                out=mvb[:, g].rearrange("p j k -> p (j k)"),
                in_=mv_bytes.rearrange("(g p j) k -> g p (j k)", p=P, j=J)[g],
            )

        for n in LOADS:
            if n[0] == "x":
                load_x(n[1], n[2])
            elif n[0] == "r":
                load_row(pairs[n[1]], n[2])
            elif n[0] == "h":
                g, q = n[1], n[2]
                nc.sync.dma_start(
                    out=mvb[:, g, 2 * q : 2 * q + 2].rearrange("p j k -> p (j k)"),
                    in_=mv_bytes.rearrange("(g p j) k -> g p j k", p=P, j=J)[g, :, 2 * q : 2 * q + 2].rearrange("p j k -> p (j k)"),
                )
            elif n[0] == "p":
                load_pair(pairs[n[1]])
            else:
                load_bytes(n[1])

        def operand(name):
            return (
                kept(name + "_i", [P, G, C, J], BF16),
                kept(name + "_c", [P, G, C], U32),
                kept(name + "_s", [P, G, C], U8),
            )

        eg, og, e1g, o1g = operand("eg"), operand("og"), operand("e1g"), operand("o1g")

        def quantize_operand(op):
            inter, codes, scales = op
            nc.vector.quantize_mx(
                out=codes[:].rearrange("p g c -> p (g c)").bitcast(FP8X4),
                scales=scales[:].rearrange("p g c -> p (g c)"),
                in_=inter[:].rearrange("p g c j -> p (g c j)"),
            )

        gain_banks = {}

        def build_diag():
            g1_cols = g1_t[:].rearrange("p g j -> p (g j)")
            for n in range(G * J):
                nc.vector.tensor_scalar(
                    out=diag[:].rearrange("p g j i -> p (g j) i")[:, n, :],
                    in0=ident_bf[:],
                    scalar1=g1_cols[:, n : n + 1],
                    scalar2=None,
                    op0=MULT,
                )

        def gain1_tensor(op, half, g):
            bank = acc_pool.tile([P, J, C], BF16, name="gain_bank", tag="acc")
            gain_banks[half, g] = bank
            for j in range(J):
                nc.tensor.matmul(
                    out=bank[:, j, :].rearrange("p (b d) -> p b d", b=B),
                    lhsT=diag[:, g, j, :],
                    rhs=x_t[:, g, :, j, half, :],
                    start=True,
                    stop=True,
                )

        def gain1_exit(op, half, g):
            nc.scalar.copy(out=op[0][:, g], in_=gain_banks[half, g][:].rearrange("p j c -> p c j"))

        def gain1_vector(op, half, g):
            nc.vector.tensor_tensor(
                out=op[0][:, g].rearrange("p (b d) j -> p b d j", b=B),
                in0=x_t[:, g, :, :, half, :].rearrange("p b j d -> p b d j"),
                in1=g1_t[:, g, :].unsqueeze(1).unsqueeze(1).to_broadcast([P, B, D, J]),
                op=MULT,
            )

        w_t, w_c, w_s, tp, acc = {}, {}, {}, {}, {}

        def widen(key, r):
            m, g, q = key
            nc.vector.tensor_tensor(
                out=raw[key][:, r, :], in0=mvb[:, g, 2 * q + r, :].bitcast(FP8), in1=mvs[:], op=MULT
            )

        def transpose(key):
            words = raw[key][:].rearrange("p r k -> p (r k)").bitcast(F32)
            for r in range(2):
                bank = tp_pool.tile([P, G, 2, P], F32, name="tp_bank")
                tp[key, r] = bank
                for g in range(G):
                    for u in range(2):
                        k0 = 512 * r + 256 * g
                        nc.tensor.transpose(bank[:, g, u, :], words[:, k0 + u : k0 + 256 : 2], ident[:])

        def copy_out(key, r, engine):
            if key not in w_t:
                w_t[key] = stage.tile([P, 2, G, P, J], BF16, name="w_t", align_bytes=64, bufs=4)
            words = w_t[key][:].rearrange("p r g c j -> p (r g c j)").bitcast(F32)
            o = words[:, 512 * r : 512 * (r + 1)].rearrange("p (g c u) -> p g c u", g=G, u=2)
            i = tp[key, r][:].rearrange("p g u c -> p g c u")
            if engine == "S":
                nc.scalar.copy(out=o, in_=i)
            else:
                nc.vector.tensor_copy(out=o, in_=i)

        def quantize_rows(key, r):
            if r == 0:
                w_c[key] = stage.tile([P, 2 * G * P], U32, name="w_c", align_bytes=64, bufs=6)
                w_s[key] = stage.tile([P, 2 * G * P], U8, name="w_s", align_bytes=64, bufs=6)
            c0 = r * G * P
            nc.vector.quantize_mx(
                out=w_c[key][:, c0 : c0 + G * P].bitcast(FP8X4),
                scales=w_s[key][:, c0 : c0 + G * P],
                in_=w_t[key][:, r].rearrange("p g c j -> p (g c j)"),
            )

        def quantize_pair(key):
            w_c[key] = stage.tile([P, 2 * G * P], U32, name="w_c", align_bytes=64, bufs=6)
            w_s[key] = stage.tile([P, 2 * G * P], U8, name="w_s", align_bytes=64, bufs=6)
            nc.vector.quantize_mx(
                out=w_c[key][:].bitcast(FP8X4), scales=w_s[key][:], in_=w_t[key][:].rearrange("p r g c j -> p (r g c j)")
            )

        rhs_of = {"mc": eg, "ma": og, "mu": o1g, "mv": e1g}

        def multiply(key, rows=(0, 1)):
            codes, scales = rhs_of[key[0]][1:]
            acc[key] = acc_pool.tile([P, 2, C], F32, name="acc_bank", tag="acc")
            extra = 1 if pairs.index(key) in EXTRA else 0
            for r in rows:
                passes = [(0, True, True)] * (extra if r == 0 else 0) + [(g, g == 0, g == G - 1) for g in range(G)]
                for g, first, final in passes:
                    c0 = (r * G + g) * P
                    nc.tensor.matmul_mx(
                        out=acc[key][:, r, :],
                        lhsT=w_c[key][:, c0 : c0 + P].bitcast(FP8X4),
                        lhsT_scale=w_s[key][:, c0 : c0 + P],
                        rhs=codes[:, g, :].bitcast(FP8X4),
                        rhs_scale=scales[:, g, :],
                        start=first,
                        stop=final,
                    )

        th = {n: kept("th_" + n, [P, G, J, C], F32) for n in ("mc", "ma", "mu", "mv")}
        act1 = {n: kept("act1_" + n, [P, G, J, C], F32) for n in ("mc", "ma")}
        half_of = {"ma": 0, "mc": 1}
        next_op = {"ma": e1g, "mc": o1g}

        def tanh(key, r0=0, r1=2):
            m, g, q = key
            nc.scalar.activation(
                out=th[m][:, g, 2 * q + r0 : 2 * q + r1, :].rearrange("p j c -> p (j c)"),
                in_=acc[key][:, r0:r1].rearrange("p j c -> p (j c)"),
                func=ACT.Tanh,
            )

        def exp(m, g):
            t = th[m][:, g].rearrange("p j c -> p (j c)")
            nc.scalar.activation(out=t, in_=t, func=ACT.Exp)

        def interact(m, g):
            nc.vector.tensor_tensor(
                out=act1[m][:, g].rearrange("p j (b d) -> p j b d", b=B),
                in0=th[m][:, g].rearrange("p j (b d) -> p j b d", b=B),
                in1=x_t[:, g, :, :, half_of[m], :].rearrange("p b j d -> p j b d"),
                op=MULT,
            )

        def gain2(m, g):
            nc.vector.tensor_tensor(
                out=next_op[m][0][:, g].rearrange("p (c i) j -> p c j i", i=4),
                in0=act1[m][:, g].rearrange("p j (c i) -> p c j i", i=4),
                in1=g2_t[:, g, :].unsqueeze(1).unsqueeze(3).to_broadcast([P, C // 4, J, 4]),
                op=MULT,
            )

        outs = {n: o.rearrange("b (g p j) d -> g p b (j d)", p=P, j=J) for n, o in (("mu", out_0), ("mv", out_1))}
        base = {"mu": "ma", "mv": "mc"}

        def finish(key, r0=0, r1=2):
            m, g, q = key
            j0, j1 = 2 * q + r0, 2 * q + r1
            res = stage.tile([P, B, r1 - r0, D], F32, name="res", bufs=4)
            nc.vector.tensor_tensor(
                out=res[:].rearrange("p b j d -> p j b d"),
                in0=act1[base[m]][:, g, j0:j1, :].rearrange("p j (b d) -> p j b d", b=B),
                in1=th[m][:, g, j0:j1, :].rearrange("p j (b d) -> p j b d", b=B),
                op=(ADD if m == "mu" else SUB),
            )
            nc.sync.dma_start(
                out=outs[m][g, :, :, j0 * D : j1 * D], in_=res[:].rearrange("p b j d -> p b (j d)")
            )

        n_pairs = len(pairs)
        last = pairs[-1]
        scratch = {}

        banks = {}

        def warm_up():
            bank = acc_pool.tile([P, 512], F32, name="warm_bank", tag="acc")
            for n in range(4):
                nc.tensor.matmul(out=bank[:], lhsT=zeros[:, :P], rhs=zeros[:], start=True, stop=True)

        def spread_scale(h):
            bank = acc_pool.tile([P, 4, P], F32, name="scale_bank", tag="acc")
            banks["scale", h] = bank
            for n in range(4):
                nc.tensor.transpose(bank[:, n, :], sc[:, 4 * h + n : 4 * h + n + 1].to_broadcast([P, P]), ident[:])

        def spread_exit(h):
            nc.scalar.copy(
                out=mvs[:].rearrange("p (k n) -> p k n", n=8)[:, :, 4 * h : 4 * h + 4],
                in_=banks["scale", h][:].rearrange("p n k -> p k n"),
            )

        def do(item):
            k = item[0]
            if k == "T":
                transpose(pairs[item[1]])
            elif k == "C":
                copy_out(pairs[item[1]], item[2], item[3])
            elif k == "Q":
                quantize_pair(pairs[item[1]])
            elif k == "q":
                quantize_rows(pairs[item[1]], item[2])
            elif k == "M":
                multiply(pairs[item[1]])
            elif k == "m":
                multiply(pairs[item[1]], (item[2],))
                acc[pairs[item[1]], item[2]] = acc[pairs[item[1]]]
            elif k == "H":
                tanh(pairs[item[1]])
            elif k == "h":
                acc[pairs[item[1]]] = acc[pairs[item[1]], item[2]]
                tanh(pairs[item[1]], item[2], item[2] + 1)
            elif k == "F":
                finish(pairs[item[1]], 0, 4 if item[1] < 14 else 2)
            elif k == "f":
                finish(pairs[item[1]], item[2], item[2] + 1)
            elif k == "X":
                exp(item[1], item[2])
            elif k == "I":
                interact(item[1], item[2])
            elif k == "G":
                gain2(item[1], item[2])
            elif k == "E":
                quantize_operand(next_op[item[1]])
            elif k == "W":
                widen(pairs[12 + item[1] // 2], item[1] % 2)
            elif k == "g":
                gain1_tensor((eg, og)[item[1]], item[1], item[2])
            elif k == "d":
                build_diag()
            elif k == "v":
                gain1_vector((eg, og)[item[1]], item[1], item[2])
            elif k == "e":
                quantize_operand((eg, og)[item[1]])
            elif k == "D":
                warm_up()
            elif k == "B":
                spread_scale(item[1])
            elif k == "b":
                spread_exit(item[1])
            elif k == "s":
                gain1_exit((eg, og)[item[1]], item[1], item[2])

        with tc.manual_schedule():
            for item in STREAM:
                do(item)
